import numpy as np
import ml_dtypes


def mxq(x, axis, fmt="e4m3"):
    dtype, down = {"e4m3": (ml_dtypes.float8_e4m3fn, 7), "e5m2": (ml_dtypes.float8_e5m2, 14)}[fmt]
    v = np.moveaxis(np.asarray(x, np.float32).astype(ml_dtypes.bfloat16).astype(np.float64), axis, -1)
    blocks = v.reshape(v.shape[:-1] + (-1, 32))
    amax = np.abs(blocks).max(-1, keepdims=True)
    byte = np.maximum(np.where(amax > 0, np.frexp(amax)[1] - 1 + 127, 0) - down, 1)
    scale = np.exp2(byte - 127.0)
    codes = (blocks / scale).astype(np.float32).astype(dtype).astype(np.float64)
    return np.moveaxis((codes * scale).reshape(v.shape), -1, axis)


WIDE = False


def mx_kscale(k):
    if not WIDE:
        return np.ones(k)
    levels = np.array([30, -30])
    if k % 512:
        return np.exp2(np.random.permutation(np.resize(levels, k // 32))).repeat(32)
    a = np.empty((k // 512, 16))
    for p in range(k // 512):
        a[p, :8] = np.random.permutation(np.resize(levels, 8))
        for g in range(8):
            far = levels[np.abs(levels - a[p, g]) >= 10]
            a[p, g + 8] = far[np.random.randint(len(far))]
    return np.exp2(a.ravel()).repeat(32)


BF16 = ml_dtypes.bfloat16


def bf(x):
    return np.asarray(x, np.float32).astype(BF16)


def f64(x):
    return np.asarray(x).astype(np.float64)


B, O, H, I = 1024, 1024, 1536, 512


def setup_inputs():
    s, t, r = mx_kscale(O), mx_kscale(H), mx_kscale(B)
    z = np.random.standard_normal((B, H))
    return {
        "u": bf(np.random.standard_normal((B, O)) * s * r[:, None]),
        "c": bf(np.random.uniform(0.5, 1.5, (B, O))),
        "w2": bf(np.random.standard_normal((H, O)) / np.sqrt(O) / s * t[:, None]),
        "d": bf(1.0 - np.tanh(z) ** 2),
        "w1": bf(np.random.standard_normal((I, H)) / np.sqrt(H) / t),
        "x": bf(np.random.standard_normal((B, I)) / np.sqrt(B) / r[:, None]),
        "v": bf(np.random.standard_normal((I, H)) * t),
        "damp": bf(np.random.uniform(0.2, 0.6, I)),
    }


def reference(u, c, w2, d, w1, x, v, damp):
    e = f64(c) * f64(u)
    dh = (mxq(e, 1, "e5m2") @ mxq(f64(w2), 1, "e4m3").T) * f64(d)
    dx = mxq(dh, 1, "e5m2") @ mxq(f64(w1), 1, "e4m3").T
    gw = mxq(f64(x), 0, "e4m3").T @ mxq(dh, 0, "e5m2")
    gw = gw + f64(damp)[:, None] * f64(v)
    return dx, gw

@@ -1,0 +1,323 @@
+from contextlib import ExitStack
+
+import concourse.mybir as mybir
+from concourse.masks import make_identity
+
+B, O, H, I = 1024, 1024, 1536, 512
+FLOPS = 2 * B * O * H + 2 * B * H * I + 2 * I * B * H
+
+F32 = mybir.dt.float32
+BF16 = mybir.dt.bfloat16
+U32 = mybir.dt.uint32
+U8 = mybir.dt.uint8
+E4M3 = mybir.dt.float8_e4m3fn_x4
+E5M2 = mybir.dt.float8_e5m2_x4
+MULT = mybir.AluOpType.mult
+ADD = mybir.AluOpType.add
+
+P = 128
+PACK = 4
+K = P * PACK
+N = 512
+W2_BUFS = 4
+UC_BUFS = 2
+E_BUFS = 4
+DH_BUFS = 4
+RES_BUFS = 8
+STAGE_BUFS = {1024: 4, 2048: 6}
+
+
+def tile_gauss_newton_pullback_s6_kernel(tc, u, c, w2, d, w1, x, v, damp, dx, gw):
+    nc = tc.nc
+    with ExitStack() as ctx:
+        keep = ctx.enter_context(tc.tile_pool(name="keep", bufs=1))
+        work = ctx.enter_context(tc.tile_pool(name="work", bufs=2))
+        psum = ctx.enter_context(tc.psum_pool(name="psum", bufs=4))
+        ctx.enter_context(tc.manual_schedule())
+
+        ident = keep.tile([P, P], F32, name="ident")
+        make_identity(nc, ident[:])
+
+        raw = {}
+        staged = {}
+        mx = {}
+        dh_rows = {}
+
+        def load(key, src, tag, bufs):
+            tile = work.tile(list(src.shape), BF16, name=tag, bufs=bufs, align_bytes=64)
+            nc.sync.dma_start(out=tile[:], in_=src)
+            raw[key] = tile
+
+        def load_w2(j, pair):
+            rows = w2[j * N + pair * 2 * P : j * N + (pair + 1) * 2 * P, :]
+            load(("w2", j, pair), rows.rearrange("(a m) o -> m a o", a=2), "w2_raw", W2_BUFS)
+
+        def load_uc(g, t0, t1):
+            for name, src in (("u", u), ("c", c)):
+                rows = src[g * K : (g + 1) * K, :].rearrange("(p t) o -> p t o", t=PACK)
+                load(name, rows[:, t0:t1, :], "%s_raw_%d" % (name, t1 - t0), UC_BUFS)
+                for t in range(t0, t1):
+                    raw[name, g, t] = raw[name][:, t - t0, :]
+
+        def load_d(g, t0, t1, j0, j1):
+            rows = d[g * K : (g + 1) * K, j0 * N : j1 * N].rearrange("(p t) h -> p t h", t=PACK)
+            load("d", rows[:, t0:t1, :], "d_raw_%d_%d_%d" % (g, t0, j0), 1)
+            for t in range(t0, t1):
+                for j in range(j0, j1):
+                    raw["d", g, j, t] = raw["d"][:, t - t0, (j - j0) * N : (j - j0 + 1) * N]
+
+        def load_w1(pair):
+            rows = w1[pair * 2 * P : (pair + 1) * 2 * P, :]
+            load(("w1", pair), rows.rearrange("(a m) h -> m a h", a=2), "w1_raw", 2)
+
+        def load_x(g):
+            load(("x", g), x[g * K : (g + 1) * K, :].rearrange("(p t) i -> p t i", t=PACK), "x_raw", 2)
+
+        def load_v():
+            load("damp", damp.rearrange("(m a) -> m a", a=PACK), "damp_raw", 1)
+            load("v", v.rearrange("(m a) h -> m a h", a=PACK), "v_raw", 1)
+
+        def stage(key, width):
+            if key not in staged:
+                staged[key] = work.tile([P, width], BF16, name="staged_%d" % width, bufs=STAGE_BUFS[width], align_bytes=64)
+            return staged[key]
+
+        def quantize(key, fmt, bufs):
+            src = staged.pop(key)
+            width = src.shape[1] // PACK
+            codes = work.tile([P, width], U32, name=key[0] + "_codes", bufs=bufs, align_bytes=64)
+            scales = work.tile([P, width], U8, name=key[0] + "_scales", bufs=bufs, align_bytes=64)
+            nc.vector.quantize_mx(out=codes[:].bitcast(fmt), scales=scales[:], in_=src[:])
+            mx[key] = (codes, scales, fmt)
+
+        def operand(key, block=None):
+            codes, scales, fmt = mx[key]
+            cols = slice(None) if block is None else slice(block * P, (block + 1) * P)
+            return codes[:, cols].bitcast(fmt), scales[:, cols]
+
+        def mx_group(pairs):
+            acc = psum.tile([P, N], F32, name="acc")
+            for n, (still, moving) in enumerate(pairs):
+                nc.tensor.matmul_mx(
+                    out=acc[:], lhsT=still[0], lhsT_scale=still[1], rhs=moving[0], rhs_scale=moving[1],
+                    start=(n == 0), stop=(n == len(pairs) - 1),
+                )
+            return acc
+
+        def turn(blocks, dst):
+            bank = psum.tile([P, 2, 2, P], F32, name="turned")
+            for s in range(2):
+                for half in range(2):
+                    nc.tensor.transpose(bank[:, s, half, :], blocks[s][half], ident[:])
+            nc.scalar.copy(out=dst.bitcast(F32).rearrange("p (s r h) -> p s r h", s=2, h=2),
+                           in_=bank[:].rearrange("p s h r -> p s r h"))
+
+        def turn_weight(name, tile, k_pass, key, pair):
+            words = [tile[:, a, :].bitcast(F32) for a in range(2)]
+            k0 = k_pass * 2 * P
+            blocks = [[words[a][:, k0 + half : k0 + 2 * P : 2] for half in range(2)] for a in range(2)]
+            turn(blocks, stage(key, 2048)[:, pair * 1024 : (pair + 1) * 1024])
+
+        def turn_w2(j, k_pass, pair):
+            turn_weight("w2", raw["w2", j, pair], k_pass, ("w2", j, k_pass), pair)
+
+        def turn_w1(j, pair):
+            turn_weight("w1", raw["w1", pair], j, ("w1", j), pair)
+
+        def make_e(g, t):
+            e = work.tile([P, O], BF16, name="e", bufs=E_BUFS, align_bytes=64)
+            pick = lambda name: raw[name, g, t].rearrange("p (m h i) -> p h m i", h=2, i=2)
+            nc.vector.tensor_tensor(out=e[:].rearrange("p (h m i) -> p h m i", h=2, i=2), in0=pick("u"), in1=pick("c"), op=MULT)
+            raw["e", g, t] = e
+
+        def turn_e(g, t):
+            words = raw["e", g, t][:].bitcast(F32)
+            blocks = [[words[:, (2 * half + s) * P : (2 * half + s + 1) * P] for half in range(2)] for s in range(2)]
+            turn(blocks, stage(("e", g, t), 1024)[:])
+
+        def make_dh(g, j, t):
+            acc = mx_group([(operand(("e", g, t), s), operand(("w2", j, s))) for s in range(2)])
+            if t == 0:
+                dh_rows[g, j] = work.tile([P, PACK, N], BF16, name="dh_rows", bufs=DH_BUFS, align_bytes=64)
+            nc.vector.tensor_tensor(
+                out=dh_rows[g, j][:, t, :].rearrange("p (h m i) -> p h m i", h=2, i=2),
+                in0=acc[:].rearrange("p (m h i) -> p h m i", h=2, i=2),
+                in1=raw["d", g, j, t].rearrange("p (m h i) -> p h m i", h=2, i=2),
+                op=MULT,
+            )
+
+        def turn_dh(g, j, pair):
+            words = [dh_rows[g, j][:, 2 * pair + s, :].bitcast(F32) for s in range(2)]
+            blocks = [[words[s][:, half * P : (half + 1) * P] for half in range(2)] for s in range(2)]
+            turn(blocks, stage(("dh_h", g, j), 2048)[:, pair * 1024 : (pair + 1) * 1024])
+
+        def weave_dh(g, j, half, copy):
+            dst = stage(("dh_b", g, j), 2048)[:].rearrange("p (q m h i t) -> p h q t m i", m=2, h=2, i=2, t=PACK)
+            src = dh_rows[g, j][:].rearrange("p t (h q m i) -> p h q t m i", h=2, m=2, i=2)
+            copy(out=dst[:, half], in_=src[:, half])
+
+        def weave(g, j, copy):
+            weave_dh(g, j, 0, copy)
+            weave_dh(g, j, 1, copy)
+
+        def weave_x(g, half, copy):
+            dst = stage(("x", g), 2048)[:].rearrange("p (a m t) -> p m t a", a=PACK, t=PACK)
+            src = raw["x", g][:].rearrange("p t (m a) -> p m t a", a=PACK)
+            cols = slice(half * P // 2, (half + 1) * P // 2)
+            copy(out=dst[:, cols], in_=src[:, cols])
+
+        def make_dx(g, t):
+            acc = mx_group([(operand(("dh_h", g, j), t), operand(("w1", j))) for j in range(3)])
+            res = work.tile([P, N], F32, name="res", bufs=RES_BUFS)
+            nc.scalar.copy(out=res[:], in_=acc[:])
+            rows = dx[g * K : (g + 1) * K, :].rearrange("(p t) i -> p t i", t=PACK)
+            nc.sync.dma_start(out=rows[:, t, :], in_=res[:])
+
+        def make_gw(j, a):
+            acc = mx_group([(operand(("x", g), a), operand(("dh_b", g, j))) for g in range(2)])
+            res = work.tile([P, N], F32, name="res", bufs=RES_BUFS)
+            cols = slice(j * N, (j + 1) * N)
+            nc.vector.scalar_tensor_tensor(out=res[:], in0=raw["v"][:, a, cols], scalar=raw["damp"][:, a : a + 1],
+                                           in1=acc[:], op0=MULT, op1=ADD)
+            nc.sync.dma_start(out=gw.rearrange("(m a) h -> m a h", a=PACK)[:, a, cols], in_=res[:])
+
+        q_w2 = lambda j, s: quantize(("w2", j, s), E4M3, 6)
+        q_e = lambda g, t: quantize(("e", g, t), E5M2, 8)
+        q_h = lambda g, j: quantize(("dh_h", g, j), E5M2, 6)
+        q_b = lambda g, j: quantize(("dh_b", g, j), E5M2, 5)
+        q_w1 = lambda j: quantize(("w1", j), E4M3, 3)
+        q_x = lambda g: quantize(("x", g), E4M3, 2)
+        S = nc.scalar.copy
+        V = nc.vector.tensor_copy
+
+        load_uc(0, 0, 1)
+        load_w2(0, 0)
+        load_w2(0, 1)
+        load_uc(0, 1, 2)
+        load_uc(0, 2, 4)
+        make_e(0, 0)
+        turn_e(0, 0)
+        turn_w2(0, 0, 0)
+        turn_w2(0, 1, 0)
+        turn_w2(0, 0, 1)
+        turn_w2(0, 1, 1)
+        load_d(0, 0, 4, 0, 1)
+        load_w2(1, 0)
+        load_w2(1, 1)
+        load_d(0, 0, 4, 1, 2)
+        load_w2(2, 0)
+        load_w2(2, 1)
+        load_d(0, 0, 4, 2, 3)
+        load_uc(1, 0, 2)
+        q_e(0, 0)
+        make_e(0, 1)
+        turn_e(0, 1)
+        q_w2(0, 0)
+        q_w2(0, 1)
+        q_e(0, 1)
+        make_e(0, 2)
+        make_e(0, 3)
+        load_uc(1, 2, 4)
+        load_d(1, 0, 2, 0, 3)
+        load_d(1, 2, 4, 0, 3)
+        load_w1(0)
+        load_w1(1)
+        load_x(0)
+        load_x(1)
+        load_v()
+        make_dh(0, 0, 0)
+        turn_e(0, 2)
+        turn_e(0, 3)
+        make_dh(0, 0, 1)
+        q_e(0, 2)
+        q_e(0, 3)
+        turn_w2(1, 0, 0)
+        turn_w2(1, 1, 0)
+        make_dh(0, 0, 2)
+        make_dh(0, 0, 3)
+        turn_w2(1, 0, 1)
+        turn_w2(1, 1, 1)
+        turn_dh(0, 0, 0)
+        turn_dh(0, 0, 1)
+        q_w2(1, 0)
+        q_w2(1, 1)
+        turn_w2(2, 0, 0)
+        turn_w2(2, 1, 0)
+        weave(0, 0, S)
+        q_h(0, 0)
+        for t in range(4):
+            make_dh(0, 1, t)
+        turn_w2(2, 0, 1)
+        turn_w2(2, 1, 1)
+        turn_dh(0, 1, 0)
+        turn_dh(0, 1, 1)
+        q_b(0, 0)
+        q_w2(2, 0)
+        q_w2(2, 1)
+        make_e(1, 0)
+        make_e(1, 1)
+        weave(0, 1, S)
+        make_dh(0, 2, 0)
+        make_dh(0, 2, 1)
+        make_e(1, 2)
+        make_e(1, 3)
+        make_dh(0, 2, 2)
+        make_dh(0, 2, 3)
+        for t in range(4):
+            turn_e(1, t)
+        turn_dh(0, 2, 0)
+        turn_dh(0, 2, 1)
+        q_h(0, 1)
+        q_e(1, 0)
+        q_e(1, 1)
+        q_b(0, 1)
+        q_e(1, 2)
+        q_e(1, 3)
+        weave(0, 2, S)
+        for t in range(4):
+            make_dh(1, 0, t)
+        turn_w1(0, 0)
+        turn_w1(1, 0)
+        turn_w1(2, 0)
+        q_h(0, 2)
+        q_b(0, 2)
+        for t in range(4):
+            make_dh(1, 1, t)
+        turn_w1(0, 1)
+        turn_w1(1, 1)
+        turn_w1(2, 1)
+        weave_x(0, 0, S)
+        weave_x(0, 1, S)
+        weave(1, 0, V)
+        q_w1(0)
+        q_w1(1)
+        q_w1(2)
+        for t in range(4):
+            make_dh(1, 2, t)
+        weave_x(1, 0, S)
+        weave_x(1, 1, S)
+        turn_dh(1, 0, 0)
+        turn_dh(1, 0, 1)
+        turn_dh(1, 1, 0)
+        turn_dh(1, 1, 1)
+        q_x(0)
+        q_b(1, 0)
+        q_x(1)
+        weave(1, 1, V)
+        for t in range(4):
+            make_dx(0, t)
+        q_h(1, 0)
+        q_b(1, 1)
+        q_h(1, 1)
+        turn_dh(1, 2, 0)
+        turn_dh(1, 2, 1)
+        weave(1, 2, S)
+        for a in range(4):
+            make_gw(0, a)
+        q_h(1, 2)
+        for a in range(4):
+            make_gw(1, a)
+            if a == 1: q_b(1, 2)
+            make_dx(1, a)
+        for t in range(4):
+            make_gw(2, t)

@@ -19,74 +19,95 @@ P = 128
 PACK = 4
 K = P * PACK
 N = 512
-W2_BUFS = 4
-UC_BUFS = 2
-E_BUFS = 4
-DH_BUFS = 4
-RES_BUFS = 8
-STAGE_BUFS = {1024: 4, 2048: 6}
+WIDE = N * PACK
+HALF = WIDE // 2
+GROUPS = B // K
+CHUNKS = H // N
+O_PASSES = O // K
+
+BUFS = {
+    "uc_row": 4, "uc_rows": 6, "w_rows": 6, "d_rows": 4, "x_rows": 1, "damp": 1, "w2_sorted": 2, "e": 4,
+    "dh_rows": 4, "result": 8,
+    "e_staged": 4, "w_staged": 3, "dh_h_staged": 8, "dh_b_staged": 2, "x_staged": 1,
+    "e_mx": 6, "w2_mx": 6, "w1_mx": 3, "dh_h_mx": 12, "dh_b_mx": 4, "x_mx": 2,
+}
+BANKS = 4
+
+BEATS = [(0, j, pair) for pair in range(2) for j in range(2)] + [(0, 2, pair) for pair in range(2)]
+BEATS = BEATS + [(1, j, pair) for j in range(CHUNKS) for pair in range(2)]
+TURN_LAG = 2
+PAIRED_FROM = 8
 
 
 def tile_gauss_newton_pullback_s6_kernel(tc, u, c, w2, d, w1, x, v, damp, dx, gw):
     nc = tc.nc
     with ExitStack() as ctx:
-        keep = ctx.enter_context(tc.tile_pool(name="keep", bufs=1))
-        work = ctx.enter_context(tc.tile_pool(name="work", bufs=2))
-        psum = ctx.enter_context(tc.psum_pool(name="psum", bufs=4))
+        sbuf = ctx.enter_context(tc.tile_pool(name="sbuf", bufs=1))
+        psum = ctx.enter_context(tc.psum_pool(name="psum", bufs=BANKS))
         ctx.enter_context(tc.manual_schedule())
 
-        ident = keep.tile([P, P], F32, name="ident")
+        ident = sbuf.tile([P, P], F32, name="ident")
         make_identity(nc, ident[:])
 
-        raw = {}
+        rows = {}
         staged = {}
         mx = {}
-        dh_rows = {}
+        banks = {}
 
-        def load(key, src, tag, bufs):
-            tile = work.tile(list(src.shape), BF16, name=tag, bufs=bufs, align_bytes=64)
-            nc.sync.dma_start(out=tile[:], in_=src)
-            raw[key] = tile
+        def tile(tag, shape, dtype, name=None):
+            return sbuf.tile(shape, dtype, name=name or tag, bufs=BUFS[tag], align_bytes=64)
 
-        def load_w2(j, pair):
-            rows = w2[j * N + pair * 2 * P : j * N + (pair + 1) * 2 * P, :]
-            load(("w2", j, pair), rows.rearrange("(a m) o -> m a o", a=2), "w2_raw", W2_BUFS)
+        def by_sample(src, g):
+            return src[g * K : (g + 1) * K, :].rearrange("(p t) w -> p t w", t=PACK)
+
+        def by_feature(src):
+            return src.rearrange("(p a) w -> p a w", a=PACK)
+
+
+        def load(tag, src):
+            dst = tile(tag, list(src.shape), BF16)
+            nc.sync.dma_start(out=dst[:], in_=src)
+            return dst
 
         def load_uc(g, t0, t1):
             for name, src in (("u", u), ("c", c)):
-                rows = src[g * K : (g + 1) * K, :].rearrange("(p t) o -> p t o", t=PACK)
-                load(name, rows[:, t0:t1, :], "%s_raw_%d" % (name, t1 - t0), UC_BUFS)
+                dst = load("uc_row" if t1 - t0 == 1 else "uc_rows", by_sample(src, g)[:, t0:t1, :])
                 for t in range(t0, t1):
-                    raw[name, g, t] = raw[name][:, t - t0, :]
+                    rows[name, g, t] = dst[:, t - t0, :]
+
+        def load_w2(j, half):
+            src = w2[j * N + half * 2 * P : j * N + (half + 1) * 2 * P, :]
+            rows["w2", j, half] = load("w_rows", src.rearrange("(a m) o -> m a o", a=2))
 
         def load_d(g, t0, t1, j0, j1):
-            rows = d[g * K : (g + 1) * K, j0 * N : j1 * N].rearrange("(p t) h -> p t h", t=PACK)
-            load("d", rows[:, t0:t1, :], "d_raw_%d_%d_%d" % (g, t0, j0), 1)
+            dst = load("d_rows", by_sample(d, g)[:, t0:t1, j0 * N : j1 * N])
             for t in range(t0, t1):
                 for j in range(j0, j1):
-                    raw["d", g, j, t] = raw["d"][:, t - t0, (j - j0) * N : (j - j0 + 1) * N]
+                    rows["d", g, j, t] = dst[:, t - t0, (j - j0) * N : (j - j0 + 1) * N]
 
-        def load_w1(pair):
-            rows = w1[pair * 2 * P : (pair + 1) * 2 * P, :]
-            load(("w1", pair), rows.rearrange("(a m) h -> m a h", a=2), "w1_raw", 2)
+        def load_w1(block):
+            rows["w1", block] = load("w_rows", w1[block * P : (block + 1) * P, :])
 
         def load_x(g):
-            load(("x", g), x[g * K : (g + 1) * K, :].rearrange("(p t) i -> p t i", t=PACK), "x_raw", 2)
+            rows["x", g] = load("x_rows", by_sample(x, g))
 
-        def load_v():
-            load("damp", damp.rearrange("(m a) -> m a", a=PACK), "damp_raw", 1)
-            load("v", v.rearrange("(m a) h -> m a h", a=PACK), "v_raw", 1)
+        def load_damping():
+            rows["damp"] = load("damp", damp.rearrange("(p a) -> p a", a=PACK))
+            for a in range(PACK):
+                rows["v", a] = load("uc_rows", by_feature(v)[:, a, :])
 
-        def stage(key, width):
+
+        def stage(key, tag, width):
             if key not in staged:
-                staged[key] = work.tile([P, width], BF16, name="staged_%d" % width, bufs=STAGE_BUFS[width], align_bytes=64)
+                staged[key] = tile(tag, [P, width], BF16)
             return staged[key]
 
-        def quantize(key, fmt, bufs):
+        def quantize(*key):
             src = staged.pop(key)
-            width = src.shape[1] // PACK
-            codes = work.tile([P, width], U32, name=key[0] + "_codes", bufs=bufs, align_bytes=64)
-            scales = work.tile([P, width], U8, name=key[0] + "_scales", bufs=bufs, align_bytes=64)
+            fmt = E5M2 if key[0] in ("e", "dh_h", "dh_b") else E4M3
+            tag = key[0] + "_mx"
+            codes = tile(tag, [P, src.shape[1] // PACK], U32, name=tag + "_codes")
+            scales = tile(tag, [P, src.shape[1] // PACK], U8, name=tag + "_scales")
             nc.vector.quantize_mx(out=codes[:].bitcast(fmt), scales=scales[:], in_=src[:])
             mx[key] = (codes, scales, fmt)
 
@@ -95,229 +116,233 @@ def tile_gauss_newton_pullback_s6_kernel(tc, u, c, w2, d, w1, x, v, damp, dx, gw
             cols = slice(None) if block is None else slice(block * P, (block + 1) * P)
             return codes[:, cols].bitcast(fmt), scales[:, cols]
 
-        def mx_group(pairs):
-            acc = psum.tile([P, N], F32, name="acc")
-            for n, (still, moving) in enumerate(pairs):
+        def multiply(key, emptied_by, passes):
+            banks[key] = psum.tile([P, N], F32, name=emptied_by)
+            for n, (still, moving) in enumerate(passes):
                 nc.tensor.matmul_mx(
-                    out=acc[:], lhsT=still[0], lhsT_scale=still[1], rhs=moving[0], rhs_scale=moving[1],
-                    start=(n == 0), stop=(n == len(pairs) - 1),
+                    out=banks[key][:], lhsT=still[0], lhsT_scale=still[1], rhs=moving[0], rhs_scale=moving[1],
+                    start=(n == 0), stop=(n == len(passes) - 1),
                 )
-            return acc
+
 
         def turn(blocks, dst):
-            bank = psum.tile([P, 2, 2, P], F32, name="turned")
-            for s in range(2):
-                for half in range(2):
-                    nc.tensor.transpose(bank[:, s, half, :], blocks[s][half], ident[:])
-            nc.scalar.copy(out=dst.bitcast(F32).rearrange("p (s r h) -> p s r h", s=2, h=2),
-                           in_=bank[:].rearrange("p s h r -> p s r h"))
+            bank = psum.tile([P, 2, 2, P], F32, name="scalar_bank")
+            for n in range(2):
+                for odd in range(2):
+                    nc.tensor.transpose(bank[:, n, odd, :], blocks[n][odd], ident[:])
+            nc.scalar.copy(out=dst.bitcast(F32).rearrange("p (n r odd) -> p n r odd", n=2, odd=2),
+                           in_=bank[:].rearrange("p n odd r -> p n r odd"))
 
-        def turn_weight(name, tile, k_pass, key, pair):
-            words = [tile[:, a, :].bitcast(F32) for a in range(2)]
-            k0 = k_pass * 2 * P
-            blocks = [[words[a][:, k0 + half : k0 + 2 * P : 2] for half in range(2)] for a in range(2)]
-            turn(blocks, stage(key, 2048)[:, pair * 1024 : (pair + 1) * 1024])
+        def every_second_pair(values, s):
+            pairs = values.bitcast(F32)
+            return [pairs[:, 2 * P * s + odd : 2 * P * (s + 1) : 2] for odd in range(2)]
 
-        def turn_w2(j, k_pass, pair):
-            turn_weight("w2", raw["w2", j, pair], k_pass, ("w2", j, k_pass), pair)
+        def sorted_pairs(values, s):
+            pairs = values.bitcast(F32)
+            odd_start = pairs.shape[1] // 2
+            return [pairs[:, odd * odd_start + P * s : odd * odd_start + P * (s + 1)] for odd in range(2)]
 
-        def turn_w1(j, pair):
-            turn_weight("w1", raw["w1", pair], j, ("w1", j), pair)
+        def as_sorted(values):
+            return values.rearrange("p (odd m i) -> p odd m i", odd=2, i=2)
+
+        def as_unsorted(values):
+            return values.rearrange("p (m odd i) -> p odd m i", odd=2, i=2)
+
+        def half_of(values, half):
+            return values[:, half * HALF : (half + 1) * HALF]
+
+        def sort_w2(j, half):
+            dst = tile("w2_sorted", [P, 2, O], BF16)
+            pairs = lambda values: values[:].rearrange("p a o -> p (a o)").bitcast(F32)
+            nc.vector.tensor_copy(out=pairs(dst).rearrange("p (a odd m) -> p a odd m", a=2, odd=2),
+                                  in_=pairs(rows["w2", j, half]).rearrange("p (a m odd) -> p a odd m", a=2, odd=2))
+            rows["w2_sorted", j, half] = dst
+
+        def turn_w2(j, half):
+            for s in range(O_PASSES):
+                if ("w2_sorted", j, half) in rows:
+                    blocks = [sorted_pairs(rows["w2_sorted", j, half][:, a, :], s) for a in range(2)]
+                else:
+                    blocks = [every_second_pair(rows["w2", j, half][:, a, :], s) for a in range(2)]
+                turn(blocks, half_of(stage(("w2", j, s), "w_staged", WIDE), half))
+
+        def turn_w1(j):
+            for half in range(2):
+                blocks = [every_second_pair(rows["w1", 2 * half + a][:], j) for a in range(2)]
+                turn(blocks, half_of(stage(("w1", j), "w_staged", WIDE), half))
 
         def make_e(g, t):
-            e = work.tile([P, O], BF16, name="e", bufs=E_BUFS, align_bytes=64)
-            pick = lambda name: raw[name, g, t].rearrange("p (m h i) -> p h m i", h=2, i=2)
-            nc.vector.tensor_tensor(out=e[:].rearrange("p (h m i) -> p h m i", h=2, i=2), in0=pick("u"), in1=pick("c"), op=MULT)
-            raw["e", g, t] = e
+            e = tile("e", [P, O], BF16)
+            nc.vector.tensor_tensor(out=as_sorted(e[:]), in0=as_unsorted(rows["u", g, t]),
+                                    in1=as_unsorted(rows["c", g, t]), op=MULT)
+            rows["e", g, t] = e
 
         def turn_e(g, t):
-            words = raw["e", g, t][:].bitcast(F32)
-            blocks = [[words[:, (2 * half + s) * P : (2 * half + s + 1) * P] for half in range(2)] for s in range(2)]
-            turn(blocks, stage(("e", g, t), 1024)[:])
-
-        def make_dh(g, j, t):
-            acc = mx_group([(operand(("e", g, t), s), operand(("w2", j, s))) for s in range(2)])
-            if t == 0:
-                dh_rows[g, j] = work.tile([P, PACK, N], BF16, name="dh_rows", bufs=DH_BUFS, align_bytes=64)
-            nc.vector.tensor_tensor(
-                out=dh_rows[g, j][:, t, :].rearrange("p (h m i) -> p h m i", h=2, i=2),
-                in0=acc[:].rearrange("p (m h i) -> p h m i", h=2, i=2),
-                in1=raw["d", g, j, t].rearrange("p (m h i) -> p h m i", h=2, i=2),
-                op=MULT,
-            )
+            turn([sorted_pairs(rows["e", g, t][:], s) for s in range(O_PASSES)], stage(("e", g, t), "e_staged", HALF)[:])
 
         def turn_dh(g, j, pair):
-            words = [dh_rows[g, j][:, 2 * pair + s, :].bitcast(F32) for s in range(2)]
-            blocks = [[words[s][:, half * P : (half + 1) * P] for half in range(2)] for s in range(2)]
-            turn(blocks, stage(("dh_h", g, j), 2048)[:, pair * 1024 : (pair + 1) * 1024])
+            blocks = [sorted_pairs(rows["dh", g, j][:, 2 * pair + n, :], 0) for n in range(2)]
+            turn(blocks, stage(("dh_h", g, j, pair), "dh_h_staged", HALF)[:])
 
-        def weave_dh(g, j, half, copy):
-            dst = stage(("dh_b", g, j), 2048)[:].rearrange("p (q m h i t) -> p h q t m i", m=2, h=2, i=2, t=PACK)
-            src = dh_rows[g, j][:].rearrange("p t (h q m i) -> p h q t m i", h=2, m=2, i=2)
-            copy(out=dst[:, half], in_=src[:, half])
 
-        def weave(g, j, copy):
-            weave_dh(g, j, 0, copy)
-            weave_dh(g, j, 1, copy)
+        def weave_dh(g, j, odd, copy):
+            dst = stage(("dh_b", g, j), "dh_b_staged", WIDE)[:]
+            dst = dst.rearrange("p (q m odd i t) -> p odd q t m i", m=2, odd=2, i=2, t=PACK)
+            src = rows["dh", g, j][:].rearrange("p t (odd q m i) -> p odd q t m i", odd=2, m=2, i=2)
+            copy(out=dst[:, odd], in_=src[:, odd])
 
         def weave_x(g, half, copy):
-            dst = stage(("x", g), 2048)[:].rearrange("p (a m t) -> p m t a", a=PACK, t=PACK)
-            src = raw["x", g][:].rearrange("p t (m a) -> p m t a", a=PACK)
+            dst = stage(("x", g), "x_staged", WIDE)[:].rearrange("p (a m t) -> p m t a", a=PACK, t=PACK)
+            src = rows["x", g][:].rearrange("p t (m a) -> p m t a", a=PACK)
             cols = slice(half * P // 2, (half + 1) * P // 2)
             copy(out=dst[:, cols], in_=src[:, cols])
 
-        def make_dx(g, t):
-            acc = mx_group([(operand(("dh_h", g, j), t), operand(("w1", j))) for j in range(3)])
-            res = work.tile([P, N], F32, name="res", bufs=RES_BUFS)
-            nc.scalar.copy(out=res[:], in_=acc[:])
-            rows = dx[g * K : (g + 1) * K, :].rearrange("(p t) i -> p t i", t=PACK)
-            nc.sync.dma_start(out=rows[:, t, :], in_=res[:])
 
-        def make_gw(j, a):
-            acc = mx_group([(operand(("x", g), a), operand(("dh_b", g, j))) for g in range(2)])
-            res = work.tile([P, N], F32, name="res", bufs=RES_BUFS)
+        def multiply_dh(g, j, t):
+            multiply(("dh", g, j, t), "vector_bank",
+                     [(operand(("e", g, t), s), operand(("w2", j, s))) for s in range(O_PASSES)])
+
+        def finish_dh(g, j, t):
+            if t == 0:
+                rows["dh", g, j] = tile("dh_rows", [P, PACK, N], BF16)
+            nc.vector.tensor_tensor(out=as_sorted(rows["dh", g, j][:, t, :]), in0=as_unsorted(banks.pop(("dh", g, j, t))[:]),
+                                    in1=as_unsorted(rows["d", g, j, t]), op=MULT)
+
+        def multiply_dx(g, t):
+            multiply(("dx", g, t), "scalar_bank",
+                     [(operand(("dh_h", g, j, t // 2), t % 2), operand(("w1", j))) for j in range(CHUNKS)])
+
+        def finish_dx(g, t):
+            result = tile("result", [P, N], F32)
+            nc.scalar.copy(out=result[:], in_=banks.pop(("dx", g, t))[:])
+            nc.sync.dma_start(out=by_sample(dx, g)[:, t, :], in_=result[:])
+
+        def multiply_gw(j, a):
+            multiply(("gw", j, a), "vector_bank",
+                     [(operand(("x", g), a), operand(("dh_b", g, j))) for g in range(GROUPS)])
+
+        def finish_gw(j, a):
+            result = tile("result", [P, N], F32)
             cols = slice(j * N, (j + 1) * N)
-            nc.vector.scalar_tensor_tensor(out=res[:], in0=raw["v"][:, a, cols], scalar=raw["damp"][:, a : a + 1],
-                                           in1=acc[:], op0=MULT, op1=ADD)
-            nc.sync.dma_start(out=gw.rearrange("(m a) h -> m a h", a=PACK)[:, a, cols], in_=res[:])
+            nc.vector.scalar_tensor_tensor(out=result[:], in0=rows["v", a][:, cols], scalar=rows["damp"][:, a : a + 1],
+                                           in1=banks.pop(("gw", j, a))[:], op0=MULT, op1=ADD)
+            nc.sync.dma_start(out=by_feature(gw)[:, a, cols], in_=result[:])
 
-        q_w2 = lambda j, s: quantize(("w2", j, s), E4M3, 6)
-        q_e = lambda g, t: quantize(("e", g, t), E5M2, 8)
-        q_h = lambda g, j: quantize(("dh_h", g, j), E5M2, 6)
-        q_b = lambda g, j: quantize(("dh_b", g, j), E5M2, 5)
-        q_w1 = lambda j: quantize(("w1", j), E4M3, 3)
-        q_x = lambda g: quantize(("x", g), E4M3, 2)
-        S = nc.scalar.copy
-        V = nc.vector.tensor_copy
+        on_scalar = nc.scalar.copy
+        on_vector = nc.vector.tensor_copy
 
         load_uc(0, 0, 1)
-        load_w2(0, 0)
-        load_w2(0, 1)
         load_uc(0, 1, 2)
+        for j in range(2):
+            for half in range(2):
+                load_w2(j, half)
         load_uc(0, 2, 4)
-        make_e(0, 0)
-        turn_e(0, 0)
-        turn_w2(0, 0, 0)
-        turn_w2(0, 1, 0)
-        turn_w2(0, 0, 1)
-        turn_w2(0, 1, 1)
-        load_d(0, 0, 4, 0, 1)
-        load_w2(1, 0)
-        load_w2(1, 1)
-        load_d(0, 0, 4, 1, 2)
+        load_x(0)
+        load_d(0, 0, 2, 0, 2)
         load_w2(2, 0)
         load_w2(2, 1)
-        load_d(0, 0, 4, 2, 3)
         load_uc(1, 0, 2)
-        q_e(0, 0)
-        make_e(0, 1)
-        turn_e(0, 1)
-        q_w2(0, 0)
-        q_w2(0, 1)
-        q_e(0, 1)
+        load_d(0, 2, 4, 0, 2)
+        load_uc(1, 2, 4)
+        load_d(0, 0, 4, 2, 3)
+
+        for t in range(2):
+            make_e(0, t)
+            turn_e(0, t)
+        sort_w2(0, 0)
+        sort_w2(0, 1)
+        turn_w2(0, 0)
+        quantize("e", 0, 0)
+        sort_w2(1, 0)
+        turn_w2(0, 1)
+        quantize("e", 0, 1)
+        sort_w2(1, 1)
+        for s in range(O_PASSES):
+            quantize("w2", 0, s)
+        turn_w2(1, 0)
+        turn_w2(1, 1)
+        for block in range(PACK):
+            load_w1(block)
+        weave_x(0, 1, on_scalar)
         make_e(0, 2)
         make_e(0, 3)
-        load_uc(1, 2, 4)
-        load_d(1, 0, 2, 0, 3)
-        load_d(1, 2, 4, 0, 3)
-        load_w1(0)
-        load_w1(1)
-        load_x(0)
-        load_x(1)
-        load_v()
-        make_dh(0, 0, 0)
-        turn_e(0, 2)
-        turn_e(0, 3)
-        make_dh(0, 0, 1)
-        q_e(0, 2)
-        q_e(0, 3)
-        turn_w2(1, 0, 0)
-        turn_w2(1, 1, 0)
-        make_dh(0, 0, 2)
-        make_dh(0, 0, 3)
-        turn_w2(1, 0, 1)
-        turn_w2(1, 1, 1)
-        turn_dh(0, 0, 0)
-        turn_dh(0, 0, 1)
-        q_w2(1, 0)
-        q_w2(1, 1)
-        turn_w2(2, 0, 0)
-        turn_w2(2, 1, 0)
-        weave(0, 0, S)
-        q_h(0, 0)
-        for t in range(4):
-            make_dh(0, 1, t)
-        turn_w2(2, 0, 1)
-        turn_w2(2, 1, 1)
-        turn_dh(0, 1, 0)
-        turn_dh(0, 1, 1)
-        q_b(0, 0)
-        q_w2(2, 0)
-        q_w2(2, 1)
-        make_e(1, 0)
-        make_e(1, 1)
-        weave(0, 1, S)
-        make_dh(0, 2, 0)
-        make_dh(0, 2, 1)
-        make_e(1, 2)
-        make_e(1, 3)
-        make_dh(0, 2, 2)
-        make_dh(0, 2, 3)
-        for t in range(4):
-            turn_e(1, t)
-        turn_dh(0, 2, 0)
-        turn_dh(0, 2, 1)
-        q_h(0, 1)
-        q_e(1, 0)
-        q_e(1, 1)
-        q_b(0, 1)
-        q_e(1, 2)
-        q_e(1, 3)
-        weave(0, 2, S)
-        for t in range(4):
-            make_dh(1, 0, t)
-        turn_w1(0, 0)
-        turn_w1(1, 0)
-        turn_w1(2, 0)
-        q_h(0, 2)
-        q_b(0, 2)
-        for t in range(4):
-            make_dh(1, 1, t)
-        turn_w1(0, 1)
-        turn_w1(1, 1)
-        turn_w1(2, 1)
-        weave_x(0, 0, S)
-        weave_x(0, 1, S)
-        weave(1, 0, V)
-        q_w1(0)
-        q_w1(1)
-        q_w1(2)
-        for t in range(4):
-            make_dh(1, 2, t)
-        weave_x(1, 0, S)
-        weave_x(1, 1, S)
-        turn_dh(1, 0, 0)
-        turn_dh(1, 0, 1)
-        turn_dh(1, 1, 0)
-        turn_dh(1, 1, 1)
-        q_x(0)
-        q_b(1, 0)
-        q_x(1)
-        weave(1, 1, V)
-        for t in range(4):
-            make_dx(0, t)
-        q_h(1, 0)
-        q_b(1, 1)
-        q_h(1, 1)
-        turn_dh(1, 2, 0)
-        turn_dh(1, 2, 1)
-        weave(1, 2, S)
-        for a in range(4):
-            make_gw(0, a)
-        q_h(1, 2)
-        for a in range(4):
-            make_gw(1, a)
-            if a == 1: q_b(1, 2)
-            make_dx(1, a)
-        for t in range(4):
-            make_gw(2, t)
+        for s in range(O_PASSES):
+            quantize("w2", 1, s)
+
+        turns = [
+            [(turn_e, 0, 2), (turn_e, 0, 3)], [(turn_w2, 2, 0)], [(turn_w2, 2, 1)],
+            [(turn_e, 1, 0), (turn_e, 1, 1)], [(turn_e, 1, 2), (turn_e, 1, 3)],
+            [(turn_w1, 0)], [(turn_w1, 1)], [(turn_w1, 2)], [], [], [], [],
+        ]
+        beside = [
+            [(weave_x, 0, 0, on_scalar), (quantize, "e", 0, 2), (quantize, "e", 0, 3),
+             (load_x, 1), (load_d, 1, 0, 2, 0, 2)],
+            [(quantize, "x", 0), (make_e, 1, 0), (make_e, 1, 1), (load_d, 1, 2, 4, 0, 2)],
+            [(weave_dh, 0, 0, 0, on_scalar), (quantize, "w2", 2, 0), (quantize, "w2", 2, 1),
+             (make_e, 1, 2), (make_e, 1, 3)],
+            [(weave_dh, 0, 0, 1, on_scalar), (quantize, "e", 1, 0), (quantize, "e", 1, 1),
+             (quantize, "dh_h", 0, 0, 0), (quantize, "dh_h", 0, 1, 0), (load_d, 1, 0, 4, 2, 3), (load_damping,)],
+            [(quantize, "e", 1, 2), (quantize, "e", 1, 3), (quantize, "dh_b", 0, 0)],
+            [(weave_x, 1, 1, on_scalar), (weave_x, 1, 0, on_vector), (quantize, "w1", 0)],
+            [(weave_dh, 0, 1, 0, on_scalar), (weave_dh, 0, 1, 1, on_vector), (quantize, "x", 1)],
+            [(weave_dh, 1, 0, 0, on_scalar), (weave_dh, 1, 0, 1, on_scalar), (quantize, "dh_b", 0, 1),
+             (quantize, "dh_h", 0, 0, 1), (quantize, "dh_h", 0, 1, 1)],
+            [],
+            [(weave_dh, 1, 1, 0, on_scalar), (weave_dh, 1, 1, 1, on_scalar), (quantize, "w1", 1),
+             (quantize, "dh_b", 1, 0)],
+            [],
+            [(weave_dh, 0, 2, 0, on_scalar), (weave_dh, 0, 2, 1, on_scalar)],
+        ]
+        turned = 0
+        for n, (g, j, pair) in enumerate(BEATS):
+            for t in (2 * pair, 2 * pair + 1):
+                multiply_dh(g, j, t)
+            for step, *args in turns[n]:
+                step(*args)
+            if n < PAIRED_FROM or (n - PAIRED_FROM) % 2 == 1:
+                while turned <= n - TURN_LAG:
+                    turn_dh(*BEATS[turned])
+                    turned = turned + 1
+            for t in (2 * pair, 2 * pair + 1):
+                finish_dh(g, j, t)
+            for step, *args in beside[n]:
+                step(*args)
+
+        for a in range(PACK):
+            multiply_gw(0, a)
+        for beat in BEATS[turned:]:
+            turn_dh(*beat)
+        finish_gw(0, 0)
+        finish_gw(0, 1)
+        quantize("dh_b", 1, 1)
+        weave_dh(1, 2, 0, on_scalar)
+        finish_gw(0, 2)
+        finish_gw(0, 3)
+        quantize("w1", 2)
+        for a in range(PACK):
+            multiply_gw(1, a)
+        for pair in range(2):
+            quantize("dh_h", 0, 2, pair)
+            finish_gw(1, 2 * pair)
+            finish_gw(1, 2 * pair + 1)
+        for t in range(PACK):
+            multiply_dx(0, t)
+            finish_dx(0, t)
+        for j in range(CHUNKS):
+            quantize("dh_h", 1, j, 0)
+        weave_dh(1, 2, 1, on_vector)
+        for g in range(GROUPS):
+            quantize("dh_b", g, 2)
+        for j in range(CHUNKS):
+            quantize("dh_h", 1, j, 1)
+        for t in range(2):
+            multiply_dx(1, t)
+            finish_dx(1, t)
+        for a in range(2):
+            multiply_gw(2, a)
+            finish_gw(2, a)
+        for n in range(2, PACK):
+            multiply_dx(1, n)
+            finish_dx(1, n)
+            multiply_gw(2, n)
+            finish_gw(2, n)

@@ -26,7 +26,7 @@ CHUNKS = H // N
 O_PASSES = O // K
 
 BUFS = {
-    "uc_row": 4, "uc_rows": 6, "w_rows": 6, "d_rows": 4, "x_rows": 1, "damp": 1, "w2_sorted": 2, "e": 4,
+    "uc_row": 4, "uc_rows": 6, "w_rows": 6, "d_first": 3, "d_second": 2, "x_rows": 1, "damp": 1, "e": 4,
     "dh_rows": 4, "result": 8,
     "e_staged": 4, "w_staged": 3, "dh_h_staged": 8, "dh_b_staged": 2, "x_staged": 1,
     "e_mx": 6, "w2_mx": 6, "w1_mx": 3, "dh_h_mx": 12, "dh_b_mx": 4, "x_mx": 2,
@@ -76,11 +76,11 @@ def tile_gauss_newton_pullback_s6_kernel(tc, u, c, w2, d, w1, x, v, damp, dx, gw
                     rows[name, g, t] = dst[:, t - t0, :]
 
         def load_w2(j, half):
-            src = w2[j * N + half * 2 * P : j * N + (half + 1) * 2 * P, :]
-            rows["w2", j, half] = load("w_rows", src.rearrange("(a m) o -> m a o", a=2))
+            src = w2[j * N : (j + 1) * N, :].rearrange("(m a) o -> m a o", a=PACK)
+            rows["w2", j, half] = load("w_rows", src[:, 2 * half : 2 * half + 2, :])
 
         def load_d(g, t0, t1, j0, j1):
-            dst = load("d_rows", by_sample(d, g)[:, t0:t1, j0 * N : j1 * N])
+            dst = load("d_second" if g else "d_first", by_sample(d, g)[:, t0:t1, j0 * N : j1 * N])
             for t in range(t0, t1):
                 for j in range(j0, j1):
                     rows["d", g, j, t] = dst[:, t - t0, (j - j0) * N : (j - j0 + 1) * N]
@@ -152,7 +152,7 @@ def tile_gauss_newton_pullback_s6_kernel(tc, u, c, w2, d, w1, x, v, damp, dx, gw
             return values[:, half * HALF : (half + 1) * HALF]
 
         def sort_w2(j, half):
-            dst = tile("w2_sorted", [P, 2, O], BF16)
+            dst = tile("dh_rows", [P, 2, O], BF16)
             pairs = lambda values: values[:].rearrange("p a o -> p (a o)").bitcast(F32)
             nc.vector.tensor_copy(out=pairs(dst).rearrange("p (a odd m) -> p a odd m", a=2, odd=2),
                                   in_=pairs(rows["w2", j, half]).rearrange("p (a m odd) -> p a odd m", a=2, odd=2))
@@ -192,9 +192,10 @@ def tile_gauss_newton_pullback_s6_kernel(tc, u, c, w2, d, w1, x, v, damp, dx, gw
             copy(out=dst[:, odd], in_=src[:, odd])
 
         def weave_x(g, half, copy):
-            dst = stage(("x", g), "x_staged", WIDE)[:].rearrange("p (a m t) -> p m t a", a=PACK, t=PACK)
-            src = rows["x", g][:].rearrange("p t (m a) -> p m t a", a=PACK)
-            cols = slice(half * P // 2, (half + 1) * P // 2)
+            dst = stage(("x", g), "x_staged", WIDE)[:]
+            dst = dst.rearrange("p (a q m t) -> p q a m t", a=PACK, m=2, t=PACK)
+            src = rows["x", g][:].rearrange("p t (q m a) -> p q a m t", m=2, a=PACK)
+            cols = slice(half * P // 4, (half + 1) * P // 4)
             copy(out=dst[:, cols], in_=src[:, cols])
 
 
@@ -205,7 +206,8 @@ def tile_gauss_newton_pullback_s6_kernel(tc, u, c, w2, d, w1, x, v, damp, dx, gw
         def finish_dh(g, j, t):
             if t == 0:
                 rows["dh", g, j] = tile("dh_rows", [P, PACK, N], BF16)
-            nc.vector.tensor_tensor(out=as_sorted(rows["dh", g, j][:, t, :]), in0=as_unsorted(banks.pop(("dh", g, j, t))[:]),
+            sums = banks.pop(("dh", g, j, t))[:].rearrange("p (odd i m) -> p odd m i", odd=2, i=2)
+            nc.vector.tensor_tensor(out=as_sorted(rows["dh", g, j][:, t, :]), in0=sums,
                                     in1=as_unsorted(rows["d", g, j, t]), op=MULT)
 
         def multiply_dx(g, t):
@@ -276,16 +278,16 @@ def tile_gauss_newton_pullback_s6_kernel(tc, u, c, w2, d, w1, x, v, damp, dx, gw
         ]
         beside = [
             [(weave_x, 0, 0, on_scalar), (quantize, "e", 0, 2), (quantize, "e", 0, 3),
-             (load_x, 1), (load_d, 1, 0, 2, 0, 2)],
-            [(quantize, "x", 0), (make_e, 1, 0), (make_e, 1, 1), (load_d, 1, 2, 4, 0, 2)],
+             (load_d, 1, 0, 2, 0, 3), (load_x, 1), (load_d, 1, 2, 4, 0, 3)],
+            [(quantize, "x", 0), (make_e, 1, 0), (make_e, 1, 1), (load_damping,)],
             [(weave_dh, 0, 0, 0, on_scalar), (quantize, "w2", 2, 0), (quantize, "w2", 2, 1),
              (make_e, 1, 2), (make_e, 1, 3)],
             [(weave_dh, 0, 0, 1, on_scalar), (quantize, "e", 1, 0), (quantize, "e", 1, 1),
-             (quantize, "dh_h", 0, 0, 0), (quantize, "dh_h", 0, 1, 0), (load_d, 1, 0, 4, 2, 3), (load_damping,)],
+             (quantize, "dh_h", 0, 0, 0), (quantize, "dh_h", 0, 1, 0)],
             [(quantize, "e", 1, 2), (quantize, "e", 1, 3), (quantize, "dh_b", 0, 0)],
-            [(weave_x, 1, 1, on_scalar), (weave_x, 1, 0, on_vector), (quantize, "w1", 0)],
-            [(weave_dh, 0, 1, 0, on_scalar), (weave_dh, 0, 1, 1, on_vector), (quantize, "x", 1)],
-            [(weave_dh, 1, 0, 0, on_scalar), (weave_dh, 1, 0, 1, on_scalar), (quantize, "dh_b", 0, 1),
+            [(weave_dh, 0, 1, 0, on_scalar), (weave_dh, 0, 1, 1, on_vector), (quantize, "w1", 0)],
+            [(weave_x, 1, 1, on_scalar), (weave_x, 1, 0, on_vector), (quantize, "dh_b", 0, 1)],
+            [(weave_dh, 1, 0, 0, on_scalar), (weave_dh, 1, 0, 1, on_scalar), (quantize, "x", 1),
              (quantize, "dh_h", 0, 0, 1), (quantize, "dh_h", 0, 1, 1)],
             [],
             [(weave_dh, 1, 1, 0, on_scalar), (weave_dh, 1, 1, 1, on_scalar), (quantize, "w1", 1),

from contextlib import ExitStack

import concourse.mybir as mybir
from concourse.masks import make_identity

B, O, H, I = 1024, 1024, 1536, 512
FLOPS = 2 * B * O * H + 2 * B * H * I + 2 * I * B * H

F32 = mybir.dt.float32
BF16 = mybir.dt.bfloat16
U32 = mybir.dt.uint32
U8 = mybir.dt.uint8
E4M3 = mybir.dt.float8_e4m3fn_x4
E5M2 = mybir.dt.float8_e5m2_x4
MULT = mybir.AluOpType.mult
ADD = mybir.AluOpType.add

P = 128
PACK = 4
K = P * PACK
N = 512
WIDE = N * PACK
HALF = WIDE // 2
GROUPS = B // K
CHUNKS = H // N
O_PASSES = O // K

BUFS = {
    "uc_row": 4, "uc_rows": 6, "w_rows": 6, "d_first": 3, "d_second": 2, "x_rows": 1, "damp": 1, "e": 4,
    "dh_rows": 4, "result": 8,
    "e_staged": 4, "w_staged": 3, "dh_h_staged": 8, "dh_b_staged": 2, "x_staged": 1,
    "e_mx": 6, "w2_mx": 6, "w1_mx": 3, "dh_h_mx": 12, "dh_b_mx": 4, "x_mx": 2,
}
BANKS = 4

BEATS = [(0, j, pair) for pair in range(2) for j in range(2)] + [(0, 2, pair) for pair in range(2)]
BEATS = BEATS + [(1, j, pair) for j in range(CHUNKS) for pair in range(2)]
TURN_LAG = 2
PAIRED_FROM = 8


def tile_gauss_newton_pullback_s6_kernel(tc, u, c, w2, d, w1, x, v, damp, dx, gw):
    nc = tc.nc
    with ExitStack() as ctx:
        sbuf = ctx.enter_context(tc.tile_pool(name="sbuf", bufs=1))
        psum = ctx.enter_context(tc.psum_pool(name="psum", bufs=BANKS))
        ctx.enter_context(tc.manual_schedule())

        ident = sbuf.tile([P, P], F32, name="ident")
        make_identity(nc, ident[:])

        rows = {}
        staged = {}
        mx = {}
        banks = {}

        def tile(tag, shape, dtype, name=None):
            return sbuf.tile(shape, dtype, name=name or tag, bufs=BUFS[tag], align_bytes=64)

        def by_sample(src, g):
            return src[g * K : (g + 1) * K, :].rearrange("(p t) w -> p t w", t=PACK)

        def by_feature(src):
            return src.rearrange("(p a) w -> p a w", a=PACK)


        def load(tag, src):
            dst = tile(tag, list(src.shape), BF16)
            nc.sync.dma_start(out=dst[:], in_=src)
            return dst

        def load_uc(g, t0, t1):
            for name, src in (("u", u), ("c", c)):
                dst = load("uc_row" if t1 - t0 == 1 else "uc_rows", by_sample(src, g)[:, t0:t1, :])
                for t in range(t0, t1):
                    rows[name, g, t] = dst[:, t - t0, :]

        def load_w2(j, half):
            src = w2[j * N : (j + 1) * N, :].rearrange("(m a) o -> m a o", a=PACK)
            rows["w2", j, half] = load("w_rows", src[:, 2 * half : 2 * half + 2, :])

        def load_d(g, t0, t1, j0, j1):
            dst = load("d_second" if g else "d_first", by_sample(d, g)[:, t0:t1, j0 * N : j1 * N])
            for t in range(t0, t1):
                for j in range(j0, j1):
                    rows["d", g, j, t] = dst[:, t - t0, (j - j0) * N : (j - j0 + 1) * N]

        def load_w1(block):
            rows["w1", block] = load("w_rows", w1[block * P : (block + 1) * P, :])

        def load_x(g):
            rows["x", g] = load("x_rows", by_sample(x, g))

        def load_damping():
            rows["damp"] = load("damp", damp.rearrange("(p a) -> p a", a=PACK))
            for a in range(PACK):
                rows["v", a] = load("uc_rows", by_feature(v)[:, a, :])


        def stage(key, tag, width):
            if key not in staged:
                staged[key] = tile(tag, [P, width], BF16)
            return staged[key]

        def quantize(*key):
            src = staged.pop(key)
            fmt = E5M2 if key[0] in ("e", "dh_h", "dh_b") else E4M3
            tag = key[0] + "_mx"
            codes = tile(tag, [P, src.shape[1] // PACK], U32, name=tag + "_codes")
            scales = tile(tag, [P, src.shape[1] // PACK], U8, name=tag + "_scales")
            nc.vector.quantize_mx(out=codes[:].bitcast(fmt), scales=scales[:], in_=src[:])
            mx[key] = (codes, scales, fmt)

        def operand(key, block=None):
            codes, scales, fmt = mx[key]
            cols = slice(None) if block is None else slice(block * P, (block + 1) * P)
            return codes[:, cols].bitcast(fmt), scales[:, cols]

        def multiply(key, emptied_by, passes):
            banks[key] = psum.tile([P, N], F32, name=emptied_by)
            for n, (still, moving) in enumerate(passes):
                nc.tensor.matmul_mx(
                    out=banks[key][:], lhsT=still[0], lhsT_scale=still[1], rhs=moving[0], rhs_scale=moving[1],
                    start=(n == 0), stop=(n == len(passes) - 1),
                )


        def turn(blocks, dst):
            bank = psum.tile([P, 2, 2, P], F32, name="scalar_bank")
            for n in range(2):
                for odd in range(2):
                    nc.tensor.transpose(bank[:, n, odd, :], blocks[n][odd], ident[:])
            nc.scalar.copy(out=dst.bitcast(F32).rearrange("p (n r odd) -> p n r odd", n=2, odd=2),
                           in_=bank[:].rearrange("p n odd r -> p n r odd"))

        def every_second_pair(values, s):
            pairs = values.bitcast(F32)
            return [pairs[:, 2 * P * s + odd : 2 * P * (s + 1) : 2] for odd in range(2)]

        def sorted_pairs(values, s):
            pairs = values.bitcast(F32)
            odd_start = pairs.shape[1] // 2
            return [pairs[:, odd * odd_start + P * s : odd * odd_start + P * (s + 1)] for odd in range(2)]

        def as_sorted(values):
            return values.rearrange("p (odd m i) -> p odd m i", odd=2, i=2)

        def as_unsorted(values):
            return values.rearrange("p (m odd i) -> p odd m i", odd=2, i=2)

        def half_of(values, half):
            return values[:, half * HALF : (half + 1) * HALF]

        def sort_w2(j, half):
            dst = tile("dh_rows", [P, 2, O], BF16)
            pairs = lambda values: values[:].rearrange("p a o -> p (a o)").bitcast(F32)
            nc.vector.tensor_copy(out=pairs(dst).rearrange("p (a odd m) -> p a odd m", a=2, odd=2),
                                  in_=pairs(rows["w2", j, half]).rearrange("p (a m odd) -> p a odd m", a=2, odd=2))
            rows["w2_sorted", j, half] = dst

        def turn_w2(j, half):
            for s in range(O_PASSES):
                if ("w2_sorted", j, half) in rows:
                    blocks = [sorted_pairs(rows["w2_sorted", j, half][:, a, :], s) for a in range(2)]
                else:
                    blocks = [every_second_pair(rows["w2", j, half][:, a, :], s) for a in range(2)]
                turn(blocks, half_of(stage(("w2", j, s), "w_staged", WIDE), half))

        def turn_w1(j):
            for half in range(2):
                blocks = [every_second_pair(rows["w1", 2 * half + a][:], j) for a in range(2)]
                turn(blocks, half_of(stage(("w1", j), "w_staged", WIDE), half))

        def make_e(g, t):
            e = tile("e", [P, O], BF16)
            nc.vector.tensor_tensor(out=as_sorted(e[:]), in0=as_unsorted(rows["u", g, t]),
                                    in1=as_unsorted(rows["c", g, t]), op=MULT)
            rows["e", g, t] = e

        def turn_e(g, t):
            turn([sorted_pairs(rows["e", g, t][:], s) for s in range(O_PASSES)], stage(("e", g, t), "e_staged", HALF)[:])

        def turn_dh(g, j, pair):
            blocks = [sorted_pairs(rows["dh", g, j][:, 2 * pair + n, :], 0) for n in range(2)]
            turn(blocks, stage(("dh_h", g, j, pair), "dh_h_staged", HALF)[:])


        def weave_dh(g, j, odd, copy):
            dst = stage(("dh_b", g, j), "dh_b_staged", WIDE)[:]
            dst = dst.rearrange("p (q m odd i t) -> p odd q t m i", m=2, odd=2, i=2, t=PACK)
            src = rows["dh", g, j][:].rearrange("p t (odd q m i) -> p odd q t m i", odd=2, m=2, i=2)
            copy(out=dst[:, odd], in_=src[:, odd])

        def weave_x(g, half, copy):
            dst = stage(("x", g), "x_staged", WIDE)[:]
            dst = dst.rearrange("p (a q m t) -> p q a m t", a=PACK, m=2, t=PACK)
            src = rows["x", g][:].rearrange("p t (q m a) -> p q a m t", m=2, a=PACK)
            cols = slice(half * P // 4, (half + 1) * P // 4)
            copy(out=dst[:, cols], in_=src[:, cols])


        def multiply_dh(g, j, t):
            multiply(("dh", g, j, t), "vector_bank",
                     [(operand(("e", g, t), s), operand(("w2", j, s))) for s in range(O_PASSES)])

        def finish_dh(g, j, t):
            if t == 0:
                rows["dh", g, j] = tile("dh_rows", [P, PACK, N], BF16)
            sums = banks.pop(("dh", g, j, t))[:].rearrange("p (odd i m) -> p odd m i", odd=2, i=2)
            nc.vector.tensor_tensor(out=as_sorted(rows["dh", g, j][:, t, :]), in0=sums,
                                    in1=as_unsorted(rows["d", g, j, t]), op=MULT)

        def multiply_dx(g, t):
            multiply(("dx", g, t), "scalar_bank",
                     [(operand(("dh_h", g, j, t // 2), t % 2), operand(("w1", j))) for j in range(CHUNKS)])

        def finish_dx(g, t):
            result = tile("result", [P, N], F32)
            nc.scalar.copy(out=result[:], in_=banks.pop(("dx", g, t))[:])
            nc.sync.dma_start(out=by_sample(dx, g)[:, t, :], in_=result[:])

        def multiply_gw(j, a):
            multiply(("gw", j, a), "vector_bank",
                     [(operand(("x", g), a), operand(("dh_b", g, j))) for g in range(GROUPS)])

        def finish_gw(j, a):
            result = tile("result", [P, N], F32)
            cols = slice(j * N, (j + 1) * N)
            nc.vector.scalar_tensor_tensor(out=result[:], in0=rows["v", a][:, cols], scalar=rows["damp"][:, a : a + 1],
                                           in1=banks.pop(("gw", j, a))[:], op0=MULT, op1=ADD)
            nc.sync.dma_start(out=by_feature(gw)[:, a, cols], in_=result[:])

        on_scalar = nc.scalar.copy
        on_vector = nc.vector.tensor_copy

        load_uc(0, 0, 1)
        load_uc(0, 1, 2)
        for j in range(2):
            for half in range(2):
                load_w2(j, half)
        load_uc(0, 2, 4)
        load_x(0)
        load_d(0, 0, 2, 0, 2)
        load_w2(2, 0)
        load_w2(2, 1)
        load_uc(1, 0, 2)
        load_d(0, 2, 4, 0, 2)
        load_uc(1, 2, 4)
        load_d(0, 0, 4, 2, 3)

        for t in range(2):
            make_e(0, t)
            turn_e(0, t)
        sort_w2(0, 0)
        sort_w2(0, 1)
        turn_w2(0, 0)
        quantize("e", 0, 0)
        sort_w2(1, 0)
        turn_w2(0, 1)
        quantize("e", 0, 1)
        sort_w2(1, 1)
        for s in range(O_PASSES):
            quantize("w2", 0, s)
        turn_w2(1, 0)
        turn_w2(1, 1)
        for block in range(PACK):
            load_w1(block)
        weave_x(0, 1, on_scalar)
        make_e(0, 2)
        make_e(0, 3)
        for s in range(O_PASSES):
            quantize("w2", 1, s)

        turns = [
            [(turn_e, 0, 2), (turn_e, 0, 3)], [(turn_w2, 2, 0)], [(turn_w2, 2, 1)],
            [(turn_e, 1, 0), (turn_e, 1, 1)], [(turn_e, 1, 2), (turn_e, 1, 3)],
            [(turn_w1, 0)], [(turn_w1, 1)], [(turn_w1, 2)], [], [], [], [],
        ]
        beside = [
            [(weave_x, 0, 0, on_scalar), (quantize, "e", 0, 2), (quantize, "e", 0, 3),
             (load_d, 1, 0, 2, 0, 3), (load_x, 1), (load_d, 1, 2, 4, 0, 3)],
            [(quantize, "x", 0), (make_e, 1, 0), (make_e, 1, 1), (load_damping,)],
            [(weave_dh, 0, 0, 0, on_scalar), (quantize, "w2", 2, 0), (quantize, "w2", 2, 1),
             (make_e, 1, 2), (make_e, 1, 3)],
            [(weave_dh, 0, 0, 1, on_scalar), (quantize, "e", 1, 0), (quantize, "e", 1, 1),
             (quantize, "dh_h", 0, 0, 0), (quantize, "dh_h", 0, 1, 0)],
            [(quantize, "e", 1, 2), (quantize, "e", 1, 3), (quantize, "dh_b", 0, 0)],
            [(weave_dh, 0, 1, 0, on_scalar), (weave_dh, 0, 1, 1, on_vector), (quantize, "w1", 0)],
            [(weave_x, 1, 1, on_scalar), (weave_x, 1, 0, on_vector), (quantize, "dh_b", 0, 1)],
            [(weave_dh, 1, 0, 0, on_scalar), (weave_dh, 1, 0, 1, on_scalar), (quantize, "x", 1),
             (quantize, "dh_h", 0, 0, 1), (quantize, "dh_h", 0, 1, 1)],
            [],
            [(weave_dh, 1, 1, 0, on_scalar), (weave_dh, 1, 1, 1, on_scalar), (quantize, "w1", 1),
             (quantize, "dh_b", 1, 0)],
            [],
            [(weave_dh, 0, 2, 0, on_scalar), (weave_dh, 0, 2, 1, on_scalar)],
        ]
        turned = 0
        for n, (g, j, pair) in enumerate(BEATS):
            for t in (2 * pair, 2 * pair + 1):
                multiply_dh(g, j, t)
            for step, *args in turns[n]:
                step(*args)
            if n < PAIRED_FROM or (n - PAIRED_FROM) % 2 == 1:
                while turned <= n - TURN_LAG:
                    turn_dh(*BEATS[turned])
                    turned = turned + 1
            for t in (2 * pair, 2 * pair + 1):
                finish_dh(g, j, t)
            for step, *args in beside[n]:
                step(*args)

        for a in range(PACK):
            multiply_gw(0, a)
        for beat in BEATS[turned:]:
            turn_dh(*beat)
        finish_gw(0, 0)
        finish_gw(0, 1)
        quantize("dh_b", 1, 1)
        weave_dh(1, 2, 0, on_scalar)
        finish_gw(0, 2)
        finish_gw(0, 3)
        quantize("w1", 2)
        for a in range(PACK):
            multiply_gw(1, a)
        for pair in range(2):
            quantize("dh_h", 0, 2, pair)
            finish_gw(1, 2 * pair)
            finish_gw(1, 2 * pair + 1)
        for t in range(PACK):
            multiply_dx(0, t)
            finish_dx(0, t)
        for j in range(CHUNKS):
            quantize("dh_h", 1, j, 0)
        weave_dh(1, 2, 1, on_vector)
        for g in range(GROUPS):
            quantize("dh_b", g, 2)
        for j in range(CHUNKS):
            quantize("dh_h", 1, j, 1)
        for t in range(2):
            multiply_dx(1, t)
            finish_dx(1, t)
        for a in range(2):
            multiply_gw(2, a)
            finish_gw(2, a)
        for n in range(2, PACK):
            multiply_dx(1, n)
            finish_dx(1, n)
            multiply_gw(2, n)
            finish_gw(2, n)
